import numpy as np
import ml_dtypes


def mxq(x, axis, fmt="e4m3"):
    dtype, down = {"e4m3": (ml_dtypes.float8_e4m3fn, 7), "e5m2": (ml_dtypes.float8_e5m2, 14)}[fmt]
    v = np.moveaxis(np.asarray(x, np.float32).astype(ml_dtypes.bfloat16).astype(np.float64), axis, -1)
    blocks = v.reshape(v.shape[:-1] + (-1, 32))
    amax = np.abs(blocks).max(-1, keepdims=True)
    byte = np.maximum(np.where(amax > 0, np.frexp(amax)[1] - 1 + 127, 0) - down, 1)
    scale = np.exp2(byte - 127.0)
    codes = (blocks / scale).astype(np.float32).astype(dtype).astype(np.float64)
    return np.moveaxis((codes * scale).reshape(v.shape), -1, axis)


WIDE = False


def mx_kscale(k):
    if not WIDE:
        return np.ones(k)
    levels = np.array([10, -10, 5, -5, 0])
    if k % 512:
        return np.exp2(np.random.permutation(np.resize(levels, k // 32))).repeat(32)
    a = np.empty((k // 512, 16))
    for p in range(k // 512):
        a[p, :8] = np.random.permutation(np.resize(levels, 8))
        for g in range(8):
            far = levels[np.abs(levels - a[p, g]) >= 10]
            a[p, g + 8] = far[np.random.randint(len(far))]
    return np.exp2(a.ravel()).repeat(32)


def f64(x):
    return np.asarray(x).astype(np.float64)


E2M1 = np.array([0.0, 0.5, 1.0, 1.5, 2.0, 3.0, 4.0, 6.0, -0.0, -0.5, -1.0, -1.5, -2.0, -3.0, -4.0, -6.0])


def pack_weight(w, fmt):
    k, n = w.shape
    w = f64(np.asarray(w, np.float32).astype(ml_dtypes.bfloat16)).reshape(k // 32, 32, n)
    amax = np.abs(w).max(1)
    if fmt == "e4m3":
        byte = np.frexp(amax)[1] - 1 + 127 - 7
    else:
        mant, ex = np.frexp(amax / 6.0)
        byte = np.where(mant > 0.5, ex, ex - 1) + 127
    byte = np.clip(np.where(amax > 0, byte, 1), 1, 254)
    scaled = (w * np.exp2(127.0 - byte)[:, None, :]).reshape(k, n).astype(np.float32)
    by_word = np.ascontiguousarray(scaled.reshape(k // 512, 128, 4, n).transpose(0, 1, 3, 2))
    if fmt == "e4m3":
        words = by_word.astype(ml_dtypes.float8_e4m3fn).view(np.uint8)
    else:
        c = by_word.astype(ml_dtypes.float4_e2m1fn).view(np.uint8) & 0xF
        words = (c[..., 0::2] | (c[..., 1::2] << 4)).reshape(k // 512, 128, 2 * n)
    return np.ascontiguousarray(words), np.ascontiguousarray(byte.astype(np.uint8).reshape(k // 512, 16, n))


def unpack_weight(words, scales, fmt):
    g, _, n = scales.shape
    words = np.ascontiguousarray(words).reshape(g, 128, n, -1)
    if fmt == "e4m3":
        vals = words.view(ml_dtypes.float8_e4m3fn).astype(np.float64)
    else:
        nib = np.empty((g, 128, n, 4), np.uint8)
        nib[..., 0::2] = words & 0xF
        nib[..., 1::2] = words >> 4
        vals = E2M1[nib]
    vals = vals * np.repeat(np.exp2(scales.astype(np.float64) - 127.0), 8, axis=1)[..., None]
    return vals.transpose(0, 1, 3, 2).reshape(g * 512, n)


K, Q, V, T = 1024, 1536, 1024, 1024


def setup_inputs():
    n = np.random.standard_normal
    s = mx_kscale(K)[:, None]
    p_wq = pack_weight(n((K, Q)) / np.sqrt(K) / s, "e2m1")
    p_wk = pack_weight(n((K, V)) / np.sqrt(K) / s, "e4m3")
    return {
        "x": (n((K, T)) * s).astype(np.float32),
        "wq_words": p_wq[0],
        "wq_scales": p_wq[1],
        "wk_words": p_wk[0],
        "wk_scales": p_wk[1],
        "wv": (n((K, V)) / np.sqrt(K) / s).astype(np.float32),
    }


def reference(x, wq_words, wq_scales, wk_words, wk_scales, wv):
    x_ = mxq(f64(x), 0, "e4m3")
    wq_ = unpack_weight(wq_words, wq_scales, "e2m1")
    wk_ = unpack_weight(wk_words, wk_scales, "e4m3")
    wv_ = mxq(f64(wv), 0, "e4m3")
    return wq_.T @ x_, wk_.T @ x_, wv_.T @ x_

@@ -1,0 +1,210 @@
+from contextlib import ExitStack
+
+import concourse.mybir as mybir
+
+K, Q, V, T = 1024, 1536, 1024, 1024
+FLOPS = 2 * K * T * (Q + V + V)
+
+F32 = mybir.dt.float32
+BF16 = mybir.dt.bfloat16
+I32 = mybir.dt.int32
+U32 = mybir.dt.uint32
+U8 = mybir.dt.uint8
+FP8X4 = mybir.dt.float8_e4m3fn_x4
+FP4X4 = mybir.dt.float4_e2m1fn_x4
+
+P = 128
+PASSES = 2
+J = 4
+BLOCK = P * J
+HALF = 512
+DVE_COLS = 352
+
+
+def tile_mix_qkv3_fm_none_kernel(
+    tc, x, wq_words, wq_scales, wk_words, wk_scales, wv, out_0, out_1, out_2
+):
+    nc = tc.nc
+    with ExitStack() as ctx:
+        keep = ctx.enter_context(tc.tile_pool(name="keep", bufs=1))
+        stage = ctx.enter_context(tc.tile_pool(name="stage", bufs=6))
+        results = ctx.enter_context(tc.tile_pool(name="results", bufs=5))
+        psum = ctx.enter_context(tc.psum_pool(name="psum", bufs=8))
+        ctx.enter_context(tc.manual_schedule())
+
+        x_raw = [keep.tile([P, J, T], F32, align_bytes=64, name="x_raw%d" % g) for g in range(PASSES)]
+        wv_raw = [keep.tile([P, J, V], F32, align_bytes=64, name="wv_raw%d" % g) for g in range(PASSES)]
+        wq_raw = keep.tile([P, PASSES, 2 * Q], U8, align_bytes=64)
+        wk_raw = keep.tile([P, PASSES, V], I32, align_bytes=64)
+        wq_sraw = keep.tile([P, PASSES * Q], U8, align_bytes=64)
+        wk_sraw = keep.tile([P, PASSES * V], U8, align_bytes=64)
+        x_codes = keep.tile([P, PASSES, T], U32, align_bytes=64)
+        x_sc = keep.tile([P, PASSES, T], U8, align_bytes=64)
+        wq_codes = keep.tile([P, PASSES, 2 * Q], U8, align_bytes=64)
+        wq_sc = keep.tile([P, PASSES, Q], U8, align_bytes=64)
+        wk_codes = keep.tile([P, PASSES, V], I32, align_bytes=64)
+        wk_sc = keep.tile([P, PASSES, V], U8, align_bytes=64)
+        wv_codes = keep.tile([P, PASSES, V], U32, align_bytes=64)
+        wv_sc = keep.tile([P, PASSES, V], U8, align_bytes=64)
+
+        nc.vector.memset(wq_sraw[:].bitcast(I32), 0)
+        nc.vector.memset(wk_sraw[:].bitcast(I32), 0)
+
+        def load_scales(raw, dram):
+            for quad in range(4):
+                nc.scalar.dma_start(
+                    out=raw[32 * quad : 32 * quad + 4, :].bitcast(I32).rearrange("r (a n) -> r a n", a=PASSES),
+                    in_=dram[:, 4 * quad : 4 * quad + 4, :].bitcast(I32).rearrange("a r n -> r a n"),
+                )
+
+        nc.sync.dma_start(
+            out=wq_raw[:].rearrange("p a n -> p (a n)").bitcast(I32).rearrange("p (a n) -> p a n", a=PASSES),
+            in_=wq_words.bitcast(I32).rearrange("a p n -> p a n"),
+        )
+        load_scales(wq_sraw, wq_scales)
+        x_view = x.rearrange("(g p j) t -> g p (j t)", g=PASSES, j=J)
+        wv_view = wv.rearrange("(g p j) m -> g p (j m)", g=PASSES, j=J)
+        for g in range(PASSES):
+            nc.sync.dma_start(out=x_raw[g][:].rearrange("p j t -> p (j t)"), in_=x_view[g])
+        nc.sync.dma_start(
+            out=wk_raw[:],
+            in_=wk_words.rearrange("a p m i -> a p (m i)").bitcast(I32).rearrange("a p m -> p a m"),
+        )
+        load_scales(wk_sraw, wk_scales)
+        for g in range(PASSES):
+            nc.sync.dma_start(out=wv_raw[g][:].rearrange("p j m -> p (j m)"), in_=wv_view[g])
+
+        def permute_wq(b):
+            for a in range(PASSES):
+                cols = slice(2 * BLOCK * b, 2 * BLOCK * (b + 1))
+                nc.vector.tensor_copy(
+                    out=wq_codes[:, a, cols].rearrange("p (j m c) -> p j m c", j=J, c=2),
+                    in_=wq_raw[:, a, cols].rearrange("p (m j c) -> p j m c", j=J, c=2),
+                )
+
+        def permute_columns(dst, src, b):
+            cols = slice(BLOCK * b, BLOCK * (b + 1))
+            nc.vector.tensor_copy(
+                out=dst[:, :, cols].rearrange("p a (j m) -> p a j m", j=J),
+                in_=src[:, :, cols].rearrange("p a (m j) -> p a j m", j=J),
+            )
+
+        wq_sraw3 = wq_sraw[:].rearrange("p (a n) -> p a n", a=PASSES)
+        wk_sraw3 = wk_sraw[:].rearrange("p (a n) -> p a n", a=PASSES)
+
+        def interleave_x(g, h):
+            grouped = stage.tile([P, J * HALF], BF16, align_bytes=64, name="grouped")
+            dst = grouped[:].rearrange("p (w j) -> p w j", j=J)
+            src = x_raw[g][:, :, HALF * h : HALF * (h + 1)].rearrange("p j w -> p w j")
+            nc.vector.tensor_copy(out=dst[:, :DVE_COLS, :], in_=src[:, :DVE_COLS, :])
+            nc.scalar.copy(out=dst[:, DVE_COLS:, :], in_=src[:, DVE_COLS:, :])
+            return grouped
+
+        def quantise(codes, scales, g, part, grouped):
+            cols = slice(HALF * part, HALF * (part + 1))
+            nc.vector.quantize_mx(out=codes[:, g, cols].bitcast(FP8X4), scales=scales[:, g, cols], in_=grouped[:])
+
+        wv_grouped = {}
+
+        def interleave_wv(g, b, j, engine):
+            if j == 0:
+                grouped = stage.tile([P, J * HALF], BF16, align_bytes=64, name="grouped")
+                wv_grouped[g, b] = grouped
+            dst = wv_grouped[g, b][:, BLOCK * j : BLOCK * (j + 1)].rearrange("p (m i) -> p m i", i=4)
+            src = wv_raw[g][:, :, BLOCK * b : BLOCK * (b + 1)].rearrange("p i (m j) -> p j m i", j=J)[:, j]
+            if engine == "v":
+                nc.vector.tensor_copy(out=dst, in_=src)
+            else:
+                nc.scalar.copy(out=dst, in_=src)
+
+        def quantise_wv(g, b):
+            quantise(wv_codes, wv_sc, g, b, wv_grouped[g, b])
+
+        def stationary(which, g, b, j):
+            c = BLOCK * b + P * j
+            if which == 0:
+                return wq_codes[:, g, 2 * c : 2 * (c + P)].bitcast(FP4X4), wq_sc[:, g, c : c + P]
+            codes, sc = ((wk_codes, wk_sc), (wv_codes, wv_sc))[which - 1]
+            return codes[:, g, c : c + P].bitcast(FP8X4), sc[:, g, c : c + P]
+
+        def multiply(acc, which, g, b, j, h):
+            w, w_sc = stationary(which, g, b, j)
+            cols = slice(HALF * h, HALF * (h + 1))
+            nc.tensor.matmul_mx(
+                out=acc[:],
+                lhsT=w,
+                lhsT_scale=w_sc,
+                rhs=x_codes[:, g, cols].bitcast(FP8X4),
+                rhs_scale=x_sc[:, g, cols],
+                start=(g == 0),
+                stop=(g == PASSES - 1),
+            )
+
+        outs = (out_0, out_1, out_2)
+        blocks = [(0, b) for b in range(3)] + [(1, b) for b in range(2)] + [(2, b) for b in range(2)]
+
+        permute_wq(0)
+        permute_columns(wq_sc, wq_sraw3, 0)
+        permute_columns(wq_sc, wq_sraw3, 1)
+        g0 = [interleave_x(0, h) for h in range(2)]
+        for h in range(2):
+            quantise(x_codes, x_sc, 0, h, g0[h])
+        permute_wq(1)
+
+        accs = {}
+        for j in range(J):
+            for h in range(2):
+                acc = psum.tile([P, HALF], F32, name="acc")
+                accs[j, h] = acc
+                multiply(acc, 0, 0, 0, j, h)
+        for h in range(2):
+            quantise(x_codes, x_sc, 1, h, interleave_x(1, h))
+
+        def wv_jobs(g, b, engines):
+            return [lambda j=j, e=e: interleave_wv(g, b, j, e) for j, e in engines]
+
+        side = {
+            1: [lambda: permute_wq(2), lambda: permute_columns(wq_sc, wq_sraw3, 2)]
+            + wv_jobs(0, 0, ((0, "s"), (1, "s"))),
+            2: [lambda: permute_columns(wk_codes, wk_raw, 0), lambda: permute_columns(wk_sc, wk_sraw3, 0)]
+            + [lambda: permute_columns(wk_codes, wk_raw, 1)]
+            + wv_jobs(0, 0, ((2, "s"), (3, "s"))),
+            3: [lambda: permute_columns(wk_sc, wk_sraw3, 1), lambda: quantise_wv(0, 0)]
+            + wv_jobs(1, 0, ((0, "v"), (1, "s"), (2, "s"), (3, "v")))
+            + wv_jobs(0, 1, ((0, "s"), (1, "v"))),
+            4: [lambda: quantise_wv(1, 0)]
+            + wv_jobs(0, 1, ((2, "v"), (3, "s")))
+            + wv_jobs(1, 1, ((0, "v"), (1, "s"), (2, "v"), (3, "s")))
+            + [lambda: quantise_wv(0, 1)],
+            5: [lambda: quantise_wv(1, 1)],
+        }
+        evacuate = {1: "ssvsssvs", 2: "svssvsvs"}
+
+        for i, (which, b) in enumerate(blocks):
+            result = results.tile([P, J, T], F32, align_bytes=64)
+            jobs = side.get(i, [])
+            if i == 0:
+                banks = [(j, h) for h in range(2) for j in range(J)]
+                for j, h in banks:
+                    multiply(accs[j, h], which, 1, b, j, h)
+            else:
+                banks = [(j, h) for j in range(J) for h in range(2)]
+                for j in range(J):
+                    for h in range(2):
+                        acc = psum.tile([P, HALF], F32, name="acc")
+                        accs[j, h] = acc
+                    for g in range(PASSES):
+                        for h in range(2):
+                            multiply(accs[j, h], which, g, b, j, h)
+            for n, (j, h) in enumerate(banks):
+                dst = result[:, j, HALF * h : HALF * (h + 1)]
+                if evacuate.get(i, "svsvsvsv")[n] == "s":
+                    nc.scalar.copy(out=dst, in_=accs[j, h][:])
+                else:
+                    nc.vector.tensor_copy(out=dst, in_=accs[j, h][:])
+                if n < len(jobs):
+                    jobs[n]()
+            nc.sync.dma_start(
+                out=outs[which].rearrange("(b p j) t -> b p (j t)", p=P, j=J)[b],
+                in_=result[:].rearrange("p j t -> p (j t)"),
+            )

@@ -40,8 +40,6 @@ def tile_mix_qkv3_fm_none_kernel(
         wk_sraw = keep.tile([P, PASSES * V], U8, align_bytes=64)
         x_codes = keep.tile([P, PASSES, T], U32, align_bytes=64)
         x_sc = keep.tile([P, PASSES, T], U8, align_bytes=64)
-        wq_codes = keep.tile([P, PASSES, 2 * Q], U8, align_bytes=64)
-        wq_sc = keep.tile([P, PASSES, Q], U8, align_bytes=64)
         wk_codes = keep.tile([P, PASSES, V], I32, align_bytes=64)
         wk_sc = keep.tile([P, PASSES, V], U8, align_bytes=64)
         wv_codes = keep.tile([P, PASSES, V], U32, align_bytes=64)
@@ -74,14 +72,6 @@ def tile_mix_qkv3_fm_none_kernel(
         for g in range(PASSES):
             nc.sync.dma_start(out=wv_raw[g][:].rearrange("p j m -> p (j m)"), in_=wv_view[g])
 
-        def permute_wq(b):
-            for a in range(PASSES):
-                cols = slice(2 * BLOCK * b, 2 * BLOCK * (b + 1))
-                nc.vector.tensor_copy(
-                    out=wq_codes[:, a, cols].rearrange("p (j m c) -> p j m c", j=J, c=2),
-                    in_=wq_raw[:, a, cols].rearrange("p (m j c) -> p j m c", j=J, c=2),
-                )
-
         def permute_columns(dst, src, b):
             cols = slice(BLOCK * b, BLOCK * (b + 1))
             nc.vector.tensor_copy(
@@ -89,7 +79,6 @@ def tile_mix_qkv3_fm_none_kernel(
                 in_=src[:, :, cols].rearrange("p a (m j) -> p a j m", j=J),
             )
 
-        wq_sraw3 = wq_sraw[:].rearrange("p (a n) -> p a n", a=PASSES)
         wk_sraw3 = wk_sraw[:].rearrange("p (a n) -> p a n", a=PASSES)
 
         def interleave_x(g, h):
@@ -106,16 +95,15 @@ def tile_mix_qkv3_fm_none_kernel(
 
         wv_grouped = {}
 
-        def interleave_wv(g, b, j, engine):
+        def interleave_wv(g, b, j):
             if j == 0:
                 grouped = stage.tile([P, J * HALF], BF16, align_bytes=64, name="grouped")
                 wv_grouped[g, b] = grouped
             dst = wv_grouped[g, b][:, BLOCK * j : BLOCK * (j + 1)].rearrange("p (m i) -> p m i", i=4)
             src = wv_raw[g][:, :, BLOCK * b : BLOCK * (b + 1)].rearrange("p i (m j) -> p j m i", j=J)[:, j]
-            if engine == "v":
-                nc.vector.tensor_copy(out=dst, in_=src)
-            else:
-                nc.scalar.copy(out=dst, in_=src)
+            nc.gpsimd.tensor_scalar(
+                out=dst, in0=src, scalar1=1.0, scalar2=0.0, op0=mybir.AluOpType.mult, op1=mybir.AluOpType.add
+            )
 
         def quantise_wv(g, b):
             quantise(wv_codes, wv_sc, g, b, wv_grouped[g, b])
@@ -123,7 +111,7 @@ def tile_mix_qkv3_fm_none_kernel(
         def stationary(which, g, b, j):
             c = BLOCK * b + P * j
             if which == 0:
-                return wq_codes[:, g, 2 * c : 2 * (c + P)].bitcast(FP4X4), wq_sc[:, g, c : c + P]
+                return wq_raw[:, g, 2 * c : 2 * (c + P)].bitcast(FP4X4), wq_sraw[:, Q * g + c : Q * g + c + P]
             codes, sc = ((wk_codes, wk_sc), (wv_codes, wv_sc))[which - 1]
             return codes[:, g, c : c + P].bitcast(FP8X4), sc[:, g, c : c + P]
 
@@ -143,13 +131,9 @@ def tile_mix_qkv3_fm_none_kernel(
         outs = (out_0, out_1, out_2)
         blocks = [(0, b) for b in range(3)] + [(1, b) for b in range(2)] + [(2, b) for b in range(2)]
 
-        permute_wq(0)
-        permute_columns(wq_sc, wq_sraw3, 0)
-        permute_columns(wq_sc, wq_sraw3, 1)
         g0 = [interleave_x(0, h) for h in range(2)]
         for h in range(2):
             quantise(x_codes, x_sc, 0, h, g0[h])
-        permute_wq(1)
 
         accs = {}
         for j in range(J):
@@ -160,25 +144,16 @@ def tile_mix_qkv3_fm_none_kernel(
         for h in range(2):
             quantise(x_codes, x_sc, 1, h, interleave_x(1, h))
 
-        def wv_jobs(g, b, engines):
-            return [lambda j=j, e=e: interleave_wv(g, b, j, e) for j, e in engines]
-
         side = {
-            1: [lambda: permute_wq(2), lambda: permute_columns(wq_sc, wq_sraw3, 2)]
-            + wv_jobs(0, 0, ((0, "s"), (1, "s"))),
-            2: [lambda: permute_columns(wk_codes, wk_raw, 0), lambda: permute_columns(wk_sc, wk_sraw3, 0)]
-            + [lambda: permute_columns(wk_codes, wk_raw, 1)]
-            + wv_jobs(0, 0, ((2, "s"), (3, "s"))),
-            3: [lambda: permute_columns(wk_sc, wk_sraw3, 1), lambda: quantise_wv(0, 0)]
-            + wv_jobs(1, 0, ((0, "v"), (1, "s"), (2, "s"), (3, "v")))
-            + wv_jobs(0, 1, ((0, "s"), (1, "v"))),
-            4: [lambda: quantise_wv(1, 0)]
-            + wv_jobs(0, 1, ((2, "v"), (3, "s")))
-            + wv_jobs(1, 1, ((0, "v"), (1, "s"), (2, "v"), (3, "s")))
-            + [lambda: quantise_wv(0, 1)],
-            5: [lambda: quantise_wv(1, 1)],
+            1: [lambda: permute_columns(wk_codes, wk_raw, 0), lambda: permute_columns(wk_sc, wk_sraw3, 0)],
+            2: [lambda: permute_columns(wk_codes, wk_raw, 1), lambda: permute_columns(wk_sc, wk_sraw3, 1)],
+            3: [lambda: quantise_wv(0, 0), lambda: quantise_wv(0, 1), lambda: quantise_wv(1, 0)],
+            4: [lambda: quantise_wv(1, 1)],
         }
-        evacuate = {1: "ssvsssvs", 2: "svssvsvs"}
+        for g in range(PASSES):
+            for b in range(2):
+                for j in range(J):
+                    interleave_wv(g, b, j)
 
         for i, (which, b) in enumerate(blocks):
             result = results.tile([P, J, T], F32, align_bytes=64)
@@ -198,13 +173,18 @@ def tile_mix_qkv3_fm_none_kernel(
                             multiply(accs[j, h], which, g, b, j, h)
             for n, (j, h) in enumerate(banks):
                 dst = result[:, j, HALF * h : HALF * (h + 1)]
-                if evacuate.get(i, "svsvsvsv")[n] == "s":
+                if "svsvsvsv"[n] == "s":
                     nc.scalar.copy(out=dst, in_=accs[j, h][:])
                 else:
                     nc.vector.tensor_copy(out=dst, in_=accs[j, h][:])
                 if n < len(jobs):
                     jobs[n]()
-            nc.sync.dma_start(
-                out=outs[which].rearrange("(b p j) t -> b p (j t)", p=P, j=J)[b],
-                in_=result[:].rearrange("p j t -> p (j t)"),
-            )
+            if which == 0:
+                for j in range(J):
+                    rows = slice(BLOCK * b + P * j, BLOCK * b + P * (j + 1))
+                    nc.sync.dma_start(out=out_0[rows, :], in_=result[:, j, :])
+            else:
+                nc.sync.dma_start(
+                    out=outs[which].rearrange("(b p j) t -> b p (j t)", p=P, j=J)[b],
+                    in_=result[:].rearrange("p j t -> p (j t)"),
+                )

@@ -48,27 +48,27 @@ def tile_mix_qkv3_fm_none_kernel(
         nc.vector.memset(wq_sraw[:].bitcast(I32), 0)
         nc.vector.memset(wk_sraw[:].bitcast(I32), 0)
 
-        def load_scales(raw, dram):
+        def load_scales(engine, raw, dram):
             for quad in range(4):
-                nc.scalar.dma_start(
+                engine.dma_start(
                     out=raw[32 * quad : 32 * quad + 4, :].bitcast(I32).rearrange("r (a n) -> r a n", a=PASSES),
                     in_=dram[:, 4 * quad : 4 * quad + 4, :].bitcast(I32).rearrange("a r n -> r a n"),
                 )
 
+        x_view = x.rearrange("(g p j) t -> g p (j t)", g=PASSES, j=J)
+        wv_view = wv.rearrange("(g p j) m -> g p (j m)", g=PASSES, j=J)
+        nc.sync.dma_start(out=x_raw[0][:].rearrange("p j t -> p (j t)"), in_=x_view[0])
+        load_scales(nc.sync, wq_sraw, wq_scales)
         nc.sync.dma_start(
             out=wq_raw[:].rearrange("p a n -> p (a n)").bitcast(I32).rearrange("p (a n) -> p a n", a=PASSES),
             in_=wq_words.bitcast(I32).rearrange("a p n -> p a n"),
         )
-        load_scales(wq_sraw, wq_scales)
-        x_view = x.rearrange("(g p j) t -> g p (j t)", g=PASSES, j=J)
-        wv_view = wv.rearrange("(g p j) m -> g p (j m)", g=PASSES, j=J)
-        for g in range(PASSES):
-            nc.sync.dma_start(out=x_raw[g][:].rearrange("p j t -> p (j t)"), in_=x_view[g])
+        nc.sync.dma_start(out=x_raw[1][:].rearrange("p j t -> p (j t)"), in_=x_view[1])
         nc.sync.dma_start(
             out=wk_raw[:],
             in_=wk_words.rearrange("a p m i -> a p (m i)").bitcast(I32).rearrange("a p m -> p a m"),
         )
-        load_scales(wk_sraw, wk_scales)
+        load_scales(nc.sync, wk_sraw, wk_scales)
         for g in range(PASSES):
             nc.sync.dma_start(out=wv_raw[g][:].rearrange("p j m -> p (j m)"), in_=wv_view[g])
 
@@ -79,14 +79,22 @@ def tile_mix_qkv3_fm_none_kernel(
                 in_=src[:, :, cols].rearrange("p a (m j) -> p a j m", j=J),
             )
 
+        def permute_words(b):
+            cols = slice(BLOCK * b, BLOCK * (b + 1))
+            nc.vector.tensor_copy(
+                out=wk_codes[:, :, cols].rearrange("p a (j m) -> p a m j", j=J),
+                in_=wk_raw[:, :, cols].rearrange("p a (m j) -> p a m j", j=J),
+            )
+
         wk_sraw3 = wk_sraw[:].rearrange("p (a n) -> p a n", a=PASSES)
 
         def interleave_x(g, h):
             grouped = stage.tile([P, J * HALF], BF16, align_bytes=64, name="grouped")
-            dst = grouped[:].rearrange("p (w j) -> p w j", j=J)
-            src = x_raw[g][:, :, HALF * h : HALF * (h + 1)].rearrange("p j w -> p w j")
-            nc.vector.tensor_copy(out=dst[:, :DVE_COLS, :], in_=src[:, :DVE_COLS, :])
-            nc.scalar.copy(out=dst[:, DVE_COLS:, :], in_=src[:, DVE_COLS:, :])
+            dst = grouped[:].rearrange("p (c i t) -> p c t i", t=J, i=4)
+            src = x_raw[g][:, :, HALF * h : HALF * (h + 1)].rearrange("p t (c i) -> p c t i", i=4)
+            split = DVE_COLS // 4
+            nc.vector.tensor_copy(out=dst[:, :split], in_=src[:, :split])
+            nc.scalar.copy(out=dst[:, split:], in_=src[:, split:])
             return grouped
 
         def quantise(codes, scales, g, part, grouped):
@@ -95,15 +103,16 @@ def tile_mix_qkv3_fm_none_kernel(
 
         wv_grouped = {}
 
-        def interleave_wv(g, b, j):
-            if j == 0:
+        def interleave_wv(g, b, half):
+            if half == 0:
                 grouped = stage.tile([P, J * HALF], BF16, align_bytes=64, name="grouped")
                 wv_grouped[g, b] = grouped
-            dst = wv_grouped[g, b][:, BLOCK * j : BLOCK * (j + 1)].rearrange("p (m i) -> p m i", i=4)
-            src = wv_raw[g][:, :, BLOCK * b : BLOCK * (b + 1)].rearrange("p i (m j) -> p j m i", j=J)[:, j]
-            nc.gpsimd.tensor_scalar(
-                out=dst, in0=src, scalar1=1.0, scalar2=0.0, op0=mybir.AluOpType.mult, op1=mybir.AluOpType.add
-            )
+            dst = wv_grouped[g, b][:].rearrange("p (j m t) -> p m t j", j=J, t=J)
+            src = wv_raw[g][:, :, BLOCK * b : BLOCK * (b + 1)].rearrange("p t (m j) -> p m t j", j=J)
+            if half == 0:
+                nc.vector.tensor_copy(out=dst[:, : P // 2], in_=src[:, : P // 2])
+            else:
+                nc.scalar.copy(out=dst[:, P // 2 :], in_=src[:, P // 2 :])
 
         def quantise_wv(g, b):
             quantise(wv_codes, wv_sc, g, b, wv_grouped[g, b])
@@ -144,16 +153,20 @@ def tile_mix_qkv3_fm_none_kernel(
         for h in range(2):
             quantise(x_codes, x_sc, 1, h, interleave_x(1, h))
 
+        def wk_jobs(b):
+            return [lambda: permute_words(b), lambda: permute_columns(wk_sc, wk_sraw3, b)]
+
+        def wv_jobs(g, b):
+            return [lambda: interleave_wv(g, b, 0), lambda: interleave_wv(g, b, 1)]
+
         side = {
-            1: [lambda: permute_columns(wk_codes, wk_raw, 0), lambda: permute_columns(wk_sc, wk_sraw3, 0)],
-            2: [lambda: permute_columns(wk_codes, wk_raw, 1), lambda: permute_columns(wk_sc, wk_sraw3, 1)],
-            3: [lambda: quantise_wv(0, 0), lambda: quantise_wv(0, 1), lambda: quantise_wv(1, 0)],
-            4: [lambda: quantise_wv(1, 1)],
+            1: wk_jobs(0),
+            2: wk_jobs(1) + wv_jobs(0, 0),
+            3: [lambda: quantise_wv(0, 0)] + wv_jobs(0, 1) + wv_jobs(1, 0),
+            4: [lambda: quantise_wv(0, 1), lambda: quantise_wv(1, 0)] + wv_jobs(1, 1),
+            5: [lambda: quantise_wv(1, 1)],
         }
-        for g in range(PASSES):
-            for b in range(2):
-                for j in range(J):
-                    interleave_wv(g, b, j)
+        evacuate = {2: "svssvsvs"}
 
         for i, (which, b) in enumerate(blocks):
             result = results.tile([P, J, T], F32, align_bytes=64)
@@ -173,7 +186,7 @@ def tile_mix_qkv3_fm_none_kernel(
                             multiply(accs[j, h], which, g, b, j, h)
             for n, (j, h) in enumerate(banks):
                 dst = result[:, j, HALF * h : HALF * (h + 1)]
-                if "svsvsvsv"[n] == "s":
+                if evacuate.get(i, "svsvsvsv")[n] == "s":
                     nc.scalar.copy(out=dst, in_=accs[j, h][:])
                 else:
                     nc.vector.tensor_copy(out=dst, in_=accs[j, h][:])

@@ -18,7 +18,7 @@ PASSES = 2
 J = 4
 BLOCK = P * J
 HALF = 512
-DVE_COLS = 352
+DVE_COLS = (352, 288)
 
 
 def tile_mix_qkv3_fm_none_kernel(
@@ -36,8 +36,8 @@ def tile_mix_qkv3_fm_none_kernel(
         wv_raw = [keep.tile([P, J, V], F32, align_bytes=64, name="wv_raw%d" % g) for g in range(PASSES)]
         wq_raw = keep.tile([P, PASSES, 2 * Q], U8, align_bytes=64)
         wk_raw = keep.tile([P, PASSES, V], I32, align_bytes=64)
-        wq_sraw = keep.tile([P, PASSES * Q], U8, align_bytes=64)
-        wk_sraw = keep.tile([P, PASSES * V], U8, align_bytes=64)
+        wq_sraw = keep.tile([P, PASSES, Q], U8, align_bytes=64)
+        wk_sraw = keep.tile([P, PASSES, V], U8, align_bytes=64)
         x_codes = keep.tile([P, PASSES, T], U32, align_bytes=64)
         x_sc = keep.tile([P, PASSES, T], U8, align_bytes=64)
         wk_codes = keep.tile([P, PASSES, V], I32, align_bytes=64)
@@ -45,32 +45,34 @@ def tile_mix_qkv3_fm_none_kernel(
         wv_codes = keep.tile([P, PASSES, V], U32, align_bytes=64)
         wv_sc = keep.tile([P, PASSES, V], U8, align_bytes=64)
 
-        nc.vector.memset(wq_sraw[:].bitcast(I32), 0)
-        nc.vector.memset(wk_sraw[:].bitcast(I32), 0)
+        nc.vector.memset(wq_sraw[:].rearrange("p a n -> p (a n)").bitcast(I32), 0)
+        nc.vector.memset(wk_sraw[:].rearrange("p a n -> p (a n)").bitcast(I32), 0)
 
-        def load_scales(engine, raw, dram):
-            for quad in range(4):
-                engine.dma_start(
-                    out=raw[32 * quad : 32 * quad + 4, :].bitcast(I32).rearrange("r (a n) -> r a n", a=PASSES),
-                    in_=dram[:, 4 * quad : 4 * quad + 4, :].bitcast(I32).rearrange("a r n -> r a n"),
-                )
+        def load_scales(raw, dram, columns):
+            held = raw[:].rearrange("p a n -> p (a n)").bitcast(I32).rearrange("p (a n) -> p a n", a=PASSES)
+            rows = dram.bitcast(I32).rearrange("a (q r) n -> r q a n", r=4)
+            for r in range(4):
+                nc.sync.dma_start(out=held[r:P:32, :, columns], in_=rows[r][:, :, columns])
+
+        def load_wq_words(columns):
+            held = wq_raw[:].rearrange("p a n -> p (a n)").bitcast(I32).rearrange("p (a n) -> p a n", a=PASSES)
+            nc.sync.dma_start(out=held[:, :, columns], in_=wq_words.bitcast(I32).rearrange("a p n -> p a n")[:, :, columns])
 
         x_view = x.rearrange("(g p j) t -> g p (j t)", g=PASSES, j=J)
         wv_view = wv.rearrange("(g p j) m -> g p (j m)", g=PASSES, j=J)
         nc.sync.dma_start(out=x_raw[0][:].rearrange("p j t -> p (j t)"), in_=x_view[0])
-        load_scales(nc.sync, wq_sraw, wq_scales)
-        nc.sync.dma_start(
-            out=wq_raw[:].rearrange("p a n -> p (a n)").bitcast(I32).rearrange("p (a n) -> p a n", a=PASSES),
-            in_=wq_words.bitcast(I32).rearrange("a p n -> p a n"),
-        )
+        load_scales(wq_sraw, wq_scales, slice(0, BLOCK // 4))
+        load_wq_words(slice(0, BLOCK // 2))
         nc.sync.dma_start(out=x_raw[1][:].rearrange("p j t -> p (j t)"), in_=x_view[1])
+        load_wq_words(slice(BLOCK // 2, Q // 2))
+        load_scales(wq_sraw, wq_scales, slice(BLOCK // 4, Q // 4))
         nc.sync.dma_start(
             out=wk_raw[:],
             in_=wk_words.rearrange("a p m i -> a p (m i)").bitcast(I32).rearrange("a p m -> p a m"),
         )
-        load_scales(nc.sync, wk_sraw, wk_scales)
-        for g in range(PASSES):
-            nc.sync.dma_start(out=wv_raw[g][:].rearrange("p j m -> p (j m)"), in_=wv_view[g])
+        nc.sync.dma_start(out=wv_raw[0][:].rearrange("p j m -> p (j m)"), in_=wv_view[0])
+        load_scales(wk_sraw, wk_scales, slice(0, V // 4))
+        nc.sync.dma_start(out=wv_raw[1][:].rearrange("p j m -> p (j m)"), in_=wv_view[1])
 
         def permute_columns(dst, src, b):
             cols = slice(BLOCK * b, BLOCK * (b + 1))
@@ -86,13 +88,11 @@ def tile_mix_qkv3_fm_none_kernel(
                 in_=wk_raw[:, :, cols].rearrange("p a (m j) -> p a m j", j=J),
             )
 
-        wk_sraw3 = wk_sraw[:].rearrange("p (a n) -> p a n", a=PASSES)
-
-        def interleave_x(g, h):
+        def interleave_x(g, h, vector_columns):
             grouped = stage.tile([P, J * HALF], BF16, align_bytes=64, name="grouped")
             dst = grouped[:].rearrange("p (c i t) -> p c t i", t=J, i=4)
             src = x_raw[g][:, :, HALF * h : HALF * (h + 1)].rearrange("p t (c i) -> p c t i", i=4)
-            split = DVE_COLS // 4
+            split = vector_columns // 4
             nc.vector.tensor_copy(out=dst[:, :split], in_=src[:, :split])
             nc.scalar.copy(out=dst[:, split:], in_=src[:, split:])
             return grouped
@@ -107,12 +107,13 @@ def tile_mix_qkv3_fm_none_kernel(
             if half == 0:
                 grouped = stage.tile([P, J * HALF], BF16, align_bytes=64, name="grouped")
                 wv_grouped[g, b] = grouped
-            dst = wv_grouped[g, b][:].rearrange("p (j m t) -> p m t j", j=J, t=J)
-            src = wv_raw[g][:, :, BLOCK * b : BLOCK * (b + 1)].rearrange("p t (m j) -> p m t j", j=J)
+            c = BLOCK * b + 2 * P * half
+            dst = wv_grouped[g, b][:, 8 * P * half : 8 * P * (half + 1)].rearrange("p (j m t) -> p m t j", j=2, t=J)
+            src = wv_raw[g][:, :, c : c + 2 * P].rearrange("p t (m j) -> p m t j", j=2)
             if half == 0:
-                nc.vector.tensor_copy(out=dst[:, : P // 2], in_=src[:, : P // 2])
+                nc.vector.tensor_copy(out=dst, in_=src)
             else:
-                nc.scalar.copy(out=dst[:, P // 2 :], in_=src[:, P // 2 :])
+                nc.scalar.copy(out=dst, in_=src)
 
         def quantise_wv(g, b):
             quantise(wv_codes, wv_sc, g, b, wv_grouped[g, b])
@@ -120,7 +121,7 @@ def tile_mix_qkv3_fm_none_kernel(
         def stationary(which, g, b, j):
             c = BLOCK * b + P * j
             if which == 0:
-                return wq_raw[:, g, 2 * c : 2 * (c + P)].bitcast(FP4X4), wq_sraw[:, Q * g + c : Q * g + c + P]
+                return wq_raw[:, g, 2 * c : 2 * (c + P)].bitcast(FP4X4), wq_sraw[:, g, c : c + P]
             codes, sc = ((wk_codes, wk_sc), (wv_codes, wv_sc))[which - 1]
             return codes[:, g, c : c + P].bitcast(FP8X4), sc[:, g, c : c + P]
 
@@ -140,7 +141,7 @@ def tile_mix_qkv3_fm_none_kernel(
         outs = (out_0, out_1, out_2)
         blocks = [(0, b) for b in range(3)] + [(1, b) for b in range(2)] + [(2, b) for b in range(2)]
 
-        g0 = [interleave_x(0, h) for h in range(2)]
+        g0 = [interleave_x(0, h, DVE_COLS[h]) for h in range(2)]
         for h in range(2):
             quantise(x_codes, x_sc, 0, h, g0[h])
 
@@ -151,17 +152,14 @@ def tile_mix_qkv3_fm_none_kernel(
                 accs[j, h] = acc
                 multiply(acc, 0, 0, 0, j, h)
         for h in range(2):
-            quantise(x_codes, x_sc, 1, h, interleave_x(1, h))
-
-        def wk_jobs(b):
-            return [lambda: permute_words(b), lambda: permute_columns(wk_sc, wk_sraw3, b)]
+            quantise(x_codes, x_sc, 1, h, interleave_x(1, h, DVE_COLS[h]))
 
         def wv_jobs(g, b):
             return [lambda: interleave_wv(g, b, 0), lambda: interleave_wv(g, b, 1)]
 
         side = {
-            1: wk_jobs(0),
-            2: wk_jobs(1) + wv_jobs(0, 0),
+            1: [lambda: permute_words(0), lambda: permute_words(1)],
+            2: [lambda: permute_columns(wk_sc, wk_sraw, 0), lambda: permute_columns(wk_sc, wk_sraw, 1)] + wv_jobs(0, 0),
             3: [lambda: quantise_wv(0, 0)] + wv_jobs(0, 1) + wv_jobs(1, 0),
             4: [lambda: quantise_wv(0, 1), lambda: quantise_wv(1, 0)] + wv_jobs(1, 1),
             5: [lambda: quantise_wv(1, 1)],
@@ -196,6 +194,12 @@ def tile_mix_qkv3_fm_none_kernel(
                 for j in range(J):
                     rows = slice(BLOCK * b + P * j, BLOCK * b + P * (j + 1))
                     nc.sync.dma_start(out=out_0[rows, :], in_=result[:, j, :])
+            elif which == 2:
+                for s in range(2):
+                    nc.sync.dma_start(
+                        out=out_2.rearrange("(c p j) t -> c p (j t)", p=P, j=2)[2 * b + s],
+                        in_=result[:, 2 * s : 2 * s + 2, :].rearrange("p j t -> p (j t)"),
+                    )
             else:
                 nc.sync.dma_start(
                     out=outs[which].rearrange("(b p j) t -> b p (j t)", p=P, j=J)[b],

from contextlib import ExitStack

import concourse.mybir as mybir

K, Q, V, T = 1024, 1536, 1024, 1024
FLOPS = 2 * K * T * (Q + V + V)

F32 = mybir.dt.float32
BF16 = mybir.dt.bfloat16
I32 = mybir.dt.int32
U32 = mybir.dt.uint32
U8 = mybir.dt.uint8
FP8X4 = mybir.dt.float8_e4m3fn_x4
FP4X4 = mybir.dt.float4_e2m1fn_x4

P = 128
PASSES = 2
J = 4
BLOCK = P * J
HALF = 512
DVE_COLS = (352, 288)


def tile_mix_qkv3_fm_none_kernel(
    tc, x, wq_words, wq_scales, wk_words, wk_scales, wv, out_0, out_1, out_2
):
    nc = tc.nc
    with ExitStack() as ctx:
        keep = ctx.enter_context(tc.tile_pool(name="keep", bufs=1))
        stage = ctx.enter_context(tc.tile_pool(name="stage", bufs=6))
        results = ctx.enter_context(tc.tile_pool(name="results", bufs=5))
        psum = ctx.enter_context(tc.psum_pool(name="psum", bufs=8))
        ctx.enter_context(tc.manual_schedule())

        x_raw = [keep.tile([P, J, T], F32, align_bytes=64, name="x_raw%d" % g) for g in range(PASSES)]
        wv_raw = [keep.tile([P, J, V], F32, align_bytes=64, name="wv_raw%d" % g) for g in range(PASSES)]
        wq_raw = keep.tile([P, PASSES, 2 * Q], U8, align_bytes=64)
        wk_raw = keep.tile([P, PASSES, V], I32, align_bytes=64)
        wq_sraw = keep.tile([P, PASSES, Q], U8, align_bytes=64)
        wk_sraw = keep.tile([P, PASSES, V], U8, align_bytes=64)
        x_codes = keep.tile([P, PASSES, T], U32, align_bytes=64)
        x_sc = keep.tile([P, PASSES, T], U8, align_bytes=64)
        wk_codes = keep.tile([P, PASSES, V], I32, align_bytes=64)
        wk_sc = keep.tile([P, PASSES, V], U8, align_bytes=64)
        wv_codes = keep.tile([P, PASSES, V], U32, align_bytes=64)
        wv_sc = keep.tile([P, PASSES, V], U8, align_bytes=64)

        nc.vector.memset(wq_sraw[:].rearrange("p a n -> p (a n)").bitcast(I32), 0)
        nc.vector.memset(wk_sraw[:].rearrange("p a n -> p (a n)").bitcast(I32), 0)

        def load_scales(raw, dram, columns):
            held = raw[:].rearrange("p a n -> p (a n)").bitcast(I32).rearrange("p (a n) -> p a n", a=PASSES)
            rows = dram.bitcast(I32).rearrange("a (q r) n -> r q a n", r=4)
            for r in range(4):
                nc.sync.dma_start(out=held[r:P:32, :, columns], in_=rows[r][:, :, columns])

        def load_wq_words(columns):
            held = wq_raw[:].rearrange("p a n -> p (a n)").bitcast(I32).rearrange("p (a n) -> p a n", a=PASSES)
            nc.sync.dma_start(out=held[:, :, columns], in_=wq_words.bitcast(I32).rearrange("a p n -> p a n")[:, :, columns])

        x_view = x.rearrange("(g p j) t -> g p (j t)", g=PASSES, j=J)
        wv_view = wv.rearrange("(g p j) m -> g p (j m)", g=PASSES, j=J)
        nc.sync.dma_start(out=x_raw[0][:].rearrange("p j t -> p (j t)"), in_=x_view[0])
        load_scales(wq_sraw, wq_scales, slice(0, BLOCK // 4))
        load_wq_words(slice(0, BLOCK // 2))
        nc.sync.dma_start(out=x_raw[1][:].rearrange("p j t -> p (j t)"), in_=x_view[1])
        load_wq_words(slice(BLOCK // 2, Q // 2))
        load_scales(wq_sraw, wq_scales, slice(BLOCK // 4, Q // 4))
        nc.sync.dma_start(
            out=wk_raw[:],
            in_=wk_words.rearrange("a p m i -> a p (m i)").bitcast(I32).rearrange("a p m -> p a m"),
        )
        nc.sync.dma_start(out=wv_raw[0][:].rearrange("p j m -> p (j m)"), in_=wv_view[0])
        load_scales(wk_sraw, wk_scales, slice(0, V // 4))
        nc.sync.dma_start(out=wv_raw[1][:].rearrange("p j m -> p (j m)"), in_=wv_view[1])

        def permute_columns(dst, src, b):
            cols = slice(BLOCK * b, BLOCK * (b + 1))
            nc.vector.tensor_copy(
                out=dst[:, :, cols].rearrange("p a (j m) -> p a j m", j=J),
                in_=src[:, :, cols].rearrange("p a (m j) -> p a j m", j=J),
            )

        def permute_words(b):
            cols = slice(BLOCK * b, BLOCK * (b + 1))
            nc.vector.tensor_copy(
                out=wk_codes[:, :, cols].rearrange("p a (j m) -> p a m j", j=J),
                in_=wk_raw[:, :, cols].rearrange("p a (m j) -> p a m j", j=J),
            )

        def interleave_x(g, h, vector_columns):
            grouped = stage.tile([P, J * HALF], BF16, align_bytes=64, name="grouped")
            dst = grouped[:].rearrange("p (c i t) -> p c t i", t=J, i=4)
            src = x_raw[g][:, :, HALF * h : HALF * (h + 1)].rearrange("p t (c i) -> p c t i", i=4)
            split = vector_columns // 4
            nc.vector.tensor_copy(out=dst[:, :split], in_=src[:, :split])
            nc.scalar.copy(out=dst[:, split:], in_=src[:, split:])
            return grouped

        def quantise(codes, scales, g, part, grouped):
            cols = slice(HALF * part, HALF * (part + 1))
            nc.vector.quantize_mx(out=codes[:, g, cols].bitcast(FP8X4), scales=scales[:, g, cols], in_=grouped[:])

        wv_grouped = {}

        def interleave_wv(g, b, half):
            if half == 0:
                grouped = stage.tile([P, J * HALF], BF16, align_bytes=64, name="grouped")
                wv_grouped[g, b] = grouped
            c = BLOCK * b + 2 * P * half
            dst = wv_grouped[g, b][:, 8 * P * half : 8 * P * (half + 1)].rearrange("p (j m t) -> p m t j", j=2, t=J)
            src = wv_raw[g][:, :, c : c + 2 * P].rearrange("p t (m j) -> p m t j", j=2)
            if half == 0:
                nc.vector.tensor_copy(out=dst, in_=src)
            else:
                nc.scalar.copy(out=dst, in_=src)

        def quantise_wv(g, b):
            quantise(wv_codes, wv_sc, g, b, wv_grouped[g, b])

        def stationary(which, g, b, j):
            c = BLOCK * b + P * j
            if which == 0:
                return wq_raw[:, g, 2 * c : 2 * (c + P)].bitcast(FP4X4), wq_sraw[:, g, c : c + P]
            codes, sc = ((wk_codes, wk_sc), (wv_codes, wv_sc))[which - 1]
            return codes[:, g, c : c + P].bitcast(FP8X4), sc[:, g, c : c + P]

        def multiply(acc, which, g, b, j, h):
            w, w_sc = stationary(which, g, b, j)
            cols = slice(HALF * h, HALF * (h + 1))
            nc.tensor.matmul_mx(
                out=acc[:],
                lhsT=w,
                lhsT_scale=w_sc,
                rhs=x_codes[:, g, cols].bitcast(FP8X4),
                rhs_scale=x_sc[:, g, cols],
                start=(g == 0),
                stop=(g == PASSES - 1),
            )

        outs = (out_0, out_1, out_2)
        blocks = [(0, b) for b in range(3)] + [(1, b) for b in range(2)] + [(2, b) for b in range(2)]

        g0 = [interleave_x(0, h, DVE_COLS[h]) for h in range(2)]
        for h in range(2):
            quantise(x_codes, x_sc, 0, h, g0[h])

        accs = {}
        for j in range(J):
            for h in range(2):
                acc = psum.tile([P, HALF], F32, name="acc")
                accs[j, h] = acc
                multiply(acc, 0, 0, 0, j, h)
        for h in range(2):
            quantise(x_codes, x_sc, 1, h, interleave_x(1, h, DVE_COLS[h]))

        def wv_jobs(g, b):
            return [lambda: interleave_wv(g, b, 0), lambda: interleave_wv(g, b, 1)]

        side = {
            1: [lambda: permute_words(0), lambda: permute_words(1)],
            2: [lambda: permute_columns(wk_sc, wk_sraw, 0), lambda: permute_columns(wk_sc, wk_sraw, 1)] + wv_jobs(0, 0),
            3: [lambda: quantise_wv(0, 0)] + wv_jobs(0, 1) + wv_jobs(1, 0),
            4: [lambda: quantise_wv(0, 1), lambda: quantise_wv(1, 0)] + wv_jobs(1, 1),
            5: [lambda: quantise_wv(1, 1)],
        }
        evacuate = {2: "svssvsvs"}

        for i, (which, b) in enumerate(blocks):
            result = results.tile([P, J, T], F32, align_bytes=64)
            jobs = side.get(i, [])
            if i == 0:
                banks = [(j, h) for h in range(2) for j in range(J)]
                for j, h in banks:
                    multiply(accs[j, h], which, 1, b, j, h)
            else:
                banks = [(j, h) for j in range(J) for h in range(2)]
                for j in range(J):
                    for h in range(2):
                        acc = psum.tile([P, HALF], F32, name="acc")
                        accs[j, h] = acc
                    for g in range(PASSES):
                        for h in range(2):
                            multiply(accs[j, h], which, g, b, j, h)
            for n, (j, h) in enumerate(banks):
                dst = result[:, j, HALF * h : HALF * (h + 1)]
                if evacuate.get(i, "svsvsvsv")[n] == "s":
                    nc.scalar.copy(out=dst, in_=accs[j, h][:])
                else:
                    nc.vector.tensor_copy(out=dst, in_=accs[j, h][:])
                if n < len(jobs):
                    jobs[n]()
            if which == 0:
                for j in range(J):
                    rows = slice(BLOCK * b + P * j, BLOCK * b + P * (j + 1))
                    nc.sync.dma_start(out=out_0[rows, :], in_=result[:, j, :])
            elif which == 2:
                for s in range(2):
                    nc.sync.dma_start(
                        out=out_2.rearrange("(c p j) t -> c p (j t)", p=P, j=2)[2 * b + s],
                        in_=result[:, 2 * s : 2 * s + 2, :].rearrange("p j t -> p (j t)"),
                    )
            else:
                nc.sync.dma_start(
                    out=outs[which].rearrange("(b p j) t -> b p (j t)", p=P, j=J)[b],
                    in_=result[:].rearrange("p j t -> p (j t)"),
                )
